import numpy as np, ml_dtypes
CORES = [23,119,17,113]
N = 4
VB, TK = 1, 64
def setup_inputs(rng):
    h = rng.standard_normal((128, TK), dtype=np.float32) / 4; w = rng.standard_normal((N, 128, VB * 128), dtype=np.float32)
    a = 2 * np.pi * rng.random((TK)); s = 400 * rng.random((TK)) ** 1.5; h[0] = s * np.cos(a); h[1] = s * np.sin(a); h[2] = 150 * rng.standard_normal((TK)); w[:, 2, :] = 1 + w[:, 2, :] / 50
    a = (2 * np.pi * rng.random() + np.pi / 2 * (rng.permutation(N).reshape(N, 1, 1) + 0.5) / N - 0.5 + (np.arange(VB).reshape(1, VB, 1) + rng.random((N, VB, 128))) / VB).reshape(N, VB * 128); w[:, 0, :] = np.cos(a); w[:, 1, :] = np.sin(a)
    tgt = rng.integers(0, N * VB * 128, size=TK)
    oh = np.zeros((N * VB * 128, TK), np.float32); oh[tgt, np.arange(TK)] = 1.0
    oh = oh.reshape(N, VB, 128, TK).transpose(0, 2, 1, 3).reshape(N, 128, VB * TK)
    return {"h": np.broadcast_to(h, (N, 128, TK)).astype(ml_dtypes.bfloat16), "w": w.astype(ml_dtypes.bfloat16), "oh": oh.astype(ml_dtypes.bfloat16)}
def reference(h, w, oh):
    H, W, OH = h.astype(np.float64), w.astype(np.float64), oh.astype(np.float64)
    Z = np.concatenate([W[r].T @ H[r] for r in range(N)], axis=0)
    O = np.concatenate([OH[r][:, TK * b:TK * b + TK] for r in range(N) for b in range(VB)], axis=0)
    m = Z.max(axis=0)
    P = np.exp(Z - m); P = P / P.sum(axis=0)
    G = P - O
    d = sum(W[r] @ G[VB * 128 * r:VB * 128 * (r + 1)] for r in range(N)).astype(ml_dtypes.bfloat16)
    return {"d": np.broadcast_to(d, (N,) + d.shape)}

from concourse.bass import DstId, RemoteDMATransfer
from concourse.mybir import AluOpType, AxisListType, ActivationFunctionType

NR = 4
TK = 64
MW = 130
PITCH = 136
ENG_FAR = 4
ENG_NEAR = 4

SCRATCH = {
    "wsb": ("sbuf", [128, 128], "bfloat16"),
    "hsb": ("sbuf", [128, TK], "bfloat16"),
    "eo": ("sbuf", [128, 2 * TK], "bfloat16"),
    "ones": ("sbuf", [128, 128], "bfloat16"),
    "ident": ("sbuf", [128, 128], "bfloat16"),
    "wt1": ("sbuf", [128, PITCH], "bfloat16"),
    "dm": ("sbuf", [128, TK], "bfloat16"),
    "land": ("sbuf", [128, NR * PITCH], "bfloat16"),
    "nm": ("sbuf", [128, 1], "float32"),
    "av": ("sbuf", [128, NR], "float32"),
    "asv": ("sbuf", [128, NR], "float32"),
    "ns": ("sbuf", [128, 1], "float32"),
    "nrc": ("sbuf", [128, 1], "float32"),
    "cv": ("sbuf", [128, NR], "float32"),
    "dg": ("sbuf", [128, NR * TK], "bfloat16"),
    "dsb": ("sbuf", [128, TK], "bfloat16"),
    "zt_ps": ("psum", [128, 512], "float32"),
    "z_ps": ("psum", [128, 512], "float32"),
    "wt_ps": ("psum", [128, 1024], "bfloat16"),
    "oa_ps": ("psum", [128, 512], "float32"),
    "ob_ps": ("psum", [128, 512], "float32"),
    "d_ps": ("psum", [128, 512], "float32"),
}
SEMAPHORES = ["s_w", "s_h", "s_oh", "s_ones", "s_pad", "s_id", "s_one", "s_mm1", "s_m", "s_dm", "s_tr", "s_wt", "s_z",
              "s_e", "s_mma", "s_mmb", "s_ca", "s_cb", "arr", "s_loc", "s_nm", "s_a", "s_as", "s_ns", "s_nr", "s_c",
              "s_tp", "s_dg0", "s_dg1", "s_dg2", "s_dg3", "s_mmf", "s_out", "s_st"]


def _engines(mask):
    return [i for i in range(mask.bit_length()) if (mask >> i) & 1]


def _spread(pool, n):
    return pool[::len(pool) // n][:n]


def _to_mask(engines):
    m = 0
    for i in engines:
        m |= 1 << i
    return m


def _plan(core, cores, topo):
    far = [c for c in cores if c != core and topo.chip(c) != topo.chip(core)]
    near = [c for c in cores if c != core and topo.chip(c) == topo.chip(core)]
    used, plan = [], []
    for group, n in ((far, ENG_FAR), (near, ENG_NEAR)):
        if not group:
            continue
        pool = [i for i in _engines(topo.mask(core, group[0])) if i not in used]
        pool = _spread(pool, n * len(group))
        for k, c in enumerate(group):
            assert topo.may_write(core, c)
            mine = pool[k * n:(k + 1) * n]
            used += mine
            plan.append((c, _to_mask(mine)))
    return plan


def rank_program(g, core, T, topo):
    rank = T.rank_of(core)
    if rank is None:
        return
    S = T.sem
    mult, X = AluOpType.mult, AxisListType.X
    Exp, Copy = ActivationFunctionType.Exp, ActivationFunctionType.Copy
    pe, ve, ac, sy = g.tensor, g.vector, g.scalar, g.sync
    o = rank * PITCH
    s_cols = T.land[0:TK, 128:NR * PITCH:PITCH]
    m_cols = T.land[0:TK, 129:NR * PITCH:PITCH]
    plan = _plan(core, T.cores, topo)
    n_out = sum(len(_engines(m)) for _, m in plan)
    n_in = 0
    for c in T.cores:
        if c != core:
            n_in += sum(len(_engines(m)) for dst, m in _plan(c, T.cores, topo) if dst == core)

    sy.dma_start(T.wsb[:, :], T.w[:, :]).then_inc(S.s_w, 16)
    ac.dma_start(T.hsb[:, :], T.h[:, :]).then_inc(S.s_h, 16)
    sy.dma_start(T.eo[:, TK:2 * TK], T.oh[:, :]).then_inc(S.s_oh, 16)

    ve.memset(T.ones[:, :], 1.0).then_inc(S.s_ones, 1)
    ve.memset(T.land[64:128, o + 129:o + 130], 0.0).then_inc(S.s_pad, 1)
    g.wait_ge(S.s_ones, 1)
    g.affine_select(T.ident[:, :], T.ones[:, :], [[-1, 128]], AluOpType.is_equal, 0.0, 0, 1).then_inc(S.s_id, 1)
    ac.wait_ge(S.s_ones, 1)
    ac.activation(T.wt1[:, 128:129], T.ones[:, 0:1], Exp, scale=0.0).then_inc(S.s_one, 1)

    pe.wait_ge(S.s_w, 16)
    pe.wait_ge(S.s_h, 16)
    pe.matmul(T.zt_ps[0:TK, 0:128], T.hsb[:, :], T.wsb[:, :], start=True, stop=True).then_inc(S.s_mm1, 1)
    pe.matmul(T.z_ps[:, 0:TK], T.wsb[:, :], T.hsb[:, :], start=True, stop=False)
    pe.wait_ge(S.s_id, 1)
    pe.transpose(T.wt_ps[:, 0:128], T.wsb[:, :], T.ident[:, :]).then_inc(S.s_tr, 1)

    ve.wait_ge(S.s_mm1, 1)
    ve.tensor_reduce(T.land[0:TK, o + 129:o + 130], T.zt_ps[0:TK, 0:128], axis=X, op=AluOpType.max).then_inc(S.s_m, 1)
    ve.wait_ge(S.s_m, 1)
    ve.wait_ge(S.s_id, 1)
    ve.tensor_scalar(T.dm[0:TK, :], T.ident[0:TK, 0:TK], T.land[0:TK, o + 129:o + 130], -1.0, mult, mult).then_inc(S.s_dm, 1)
    ve.wait_ge(S.s_tr, 1)
    ve.tensor_copy(T.wt1[:, 0:128], T.wt_ps[:, 0:128]).then_inc(S.s_wt, 1)

    pe.wait_ge(S.s_dm, 1)
    pe.wait_ge(S.s_ones, 1)
    pe.matmul(T.z_ps[:, 0:TK], T.ones[0:TK, :], T.dm[0:TK, :], start=False, stop=True).then_inc(S.s_z, 1)
    ac.wait_ge(S.s_z, 1)
    ac.activation(T.eo[:, 0:TK], T.z_ps[:, 0:TK], Exp).then_inc(S.s_e, 1)

    for s in (S.s_e, S.s_wt, S.s_one):
        pe.wait_ge(s, 1)
    pe.wait_ge(S.s_oh, 16)
    pe.matmul(T.oa_ps[:, 0:64], T.eo[:, :], T.wt1[:, 0:64], start=True, stop=True).then_inc(S.s_mma, 1)
    pe.matmul(T.ob_ps[:, 0:65], T.eo[:, :], T.wt1[:, 64:129], start=True, stop=True).then_inc(S.s_mmb, 1)
    ve.wait_ge(S.s_mma, 1)
    ve.tensor_copy(T.land[:, o:o + 64], T.oa_ps[:, 0:64]).then_inc(S.s_ca, 1)
    ac.wait_ge(S.s_mmb, 1)
    ac.activation(T.land[:, o + 64:o + 129], T.ob_ps[:, 0:65], Copy).then_inc(S.s_cb, 1)

    for s in (S.s_ca, S.s_cb, S.s_m, S.s_pad):
        g.wait_ge(s, 1)
    transfers = []
    for dst, mask in plan:
        rid, pid, _ = topo.addr(dst)
        transfers.append(RemoteDMATransfer(dst_ids=[DstId(rid=rid, pnc=pid)], dma_engine_mask=mask, remote_sem=S.arr,
                                           src=T.land[:, o:o + MW], dst=T.land[:, o:o + MW]))
    g.remote_dma_fused(transfers, local_sem=S.s_loc)
    g.wait_ge(S.s_loc, n_out)

    pe.wait_ge(S.arr, n_in)
    pe.wait_ge(S.s_ca, 1)
    pe.wait_ge(S.s_cb, 1)
    for q in range(NR):
        mm = pe.matmul(T.d_ps[:, 0:TK], T.land[64:128, q * PITCH:q * PITCH + 128], T.ident[64:128, 64:128],
                       start=(q == 0), stop=False)
    mm.then_inc(S.s_tp, 1)
    pe.wait_ge(S.s_tp, 1)

    ve.wait_ge(S.arr, n_in)
    ve.wait_ge(S.s_cb, 1)
    ve.tensor_reduce(T.nm[0:TK, :], m_cols, axis=X, op=AluOpType.max, negate=True).then_inc(S.s_nm, 1)
    ac.wait_ge(S.arr, n_in)
    ac.wait_ge(S.s_m, 1)
    ac.wait_ge(S.s_nm, 1)
    ac.activation(T.av[0:TK, :], m_cols, Exp, bias=T.nm[0:TK, :]).then_inc(S.s_a, 1)
    ve.wait_ge(S.s_a, 1)
    ve.tensor_tensor(T.asv[0:TK, :], T.av[0:TK, :], s_cols, mult).then_inc(S.s_as, 1)
    ve.wait_ge(S.s_as, 1)
    ve.tensor_reduce(T.ns[0:TK, :], T.asv[0:TK, :], axis=X, op=AluOpType.add, negate=True).then_inc(S.s_ns, 1)
    ve.wait_ge(S.s_ns, 1)
    ve.reciprocal(T.nrc[0:TK, :], T.ns[0:TK, :]).then_inc(S.s_nr, 1)
    ve.wait_ge(S.s_nr, 1)
    ve.tensor_scalar(T.cv[0:TK, :], T.av[0:TK, :], T.nrc[0:TK, :], None, mult).then_inc(S.s_c, 1)

    ve.wait_ge(S.s_c, 1)
    ac.wait_ge(S.s_c, 1)
    ac.wait_ge(S.s_id, 1)
    for q in (0, 1):
        ve.tensor_scalar(T.dg[0:TK, q * TK:(q + 1) * TK], T.ident[0:TK, 0:TK], T.cv[0:TK, q:q + 1], None,
                         mult).then_inc(S["s_dg%d" % q], 1)
    for q in (2, 3):
        ac.activation(T.dg[0:TK, q * TK:(q + 1) * TK], T.ident[0:TK, 0:TK], Copy,
                      scale=T.cv[0:TK, q:q + 1]).then_inc(S["s_dg%d" % q], 1)

    order = (0, 2, 1, 3)
    for k, q in enumerate(order):
        pe.wait_ge(S["s_dg%d" % q], 1)
        mm = pe.matmul(T.d_ps[:, 0:TK], T.land[0:TK, q * PITCH:q * PITCH + 128], T.dg[0:TK, q * TK:(q + 1) * TK],
                       start=False, stop=(k == NR - 1))
    mm.then_inc(S.s_mmf, 1)
    ve.wait_ge(S.s_mmf, 1)
    ve.tensor_scalar(T.dsb[:, :], T.d_ps[:, 0:TK], -1.0, None, mult).then_inc(S.s_out, 1)
    sy.wait_ge(S.s_out, 1)
    sy.dma_start(T.d[:, :], T.dsb[:, :]).then_inc(S.s_st, 16)
    sy.wait_ge(S.s_st, 16)
